import numpy as np
import ml_dtypes

BF16 = ml_dtypes.bfloat16


def bf(x):
    return np.asarray(x, np.float32).astype(BF16)


def f32(x):
    return np.asarray(x, np.float32)


def f64(x):
    return np.asarray(x).astype(np.float64)


def striped(idx):
    return np.tile(idx.reshape(-1, 16).T, (8, 1))


S, K, M, N, E, Q = 512, 256, 128, 128, 2, 64


def setup_inputs():
    return {"base": bf(np.random.standard_normal((M, S))), "x": bf(np.random.standard_normal((K, N))), "w": bf(np.random.standard_normal((E, K, M)) / np.sqrt(K)), "offs": striped(np.random.permutation(S)[:N])}


def reference(base, x, w, offs):
    idx = offs[:16].T.reshape(-1)
    z = f64(base).copy()
    for e in range(E):
        z[:, idx[e * Q : (e + 1) * Q]] += f64(w)[e].T @ f64(x)[:, e * Q : (e + 1) * Q]
    return z

@@ -1,0 +1,54 @@
+import concourse.mybir as mybir
+from concourse.masks import make_identity
+
+BF16, F32, U16 = mybir.dt.bfloat16, mybir.dt.float32, mybir.dt.uint16
+
+P = 128
+S = 512
+K = 256
+KB = K // P
+E = 2
+Q = 64
+N = E * Q
+QC = Q // 16
+
+FLOPS = 2 * K * P * N
+
+
+def tile_scatter_matmul_kernel(tc, base, x, w, offs, out):
+    nc = tc.nc
+    with (
+        tc.tile_pool(name="held", bufs=1) as held,
+        tc.psum_pool(name="psum", bufs=1) as psum,
+    ):
+        offsets = held.tile([P, N // 16], U16, name="offsets")
+        nc.sync.dma_start(offsets[:], offs)
+
+        base_sb = held.tile([P, S], BF16, name="base_sb")
+        nc.scalar.dma_start(base_sb[:], base)
+
+        w_sb = held.tile([P, E * KB, P], BF16, name="w_sb")
+        nc.sync.dma_start(w_sb[:], w.rearrange("e (b p) m -> p (e b) m", p=P))
+        x_sb = held.tile([P, KB, N], BF16, name="x_sb")
+        nc.scalar.dma_start(x_sb[:], x.rearrange("(b p) n -> p b n", p=P))
+
+        ident = held.tile([P, P], BF16, name="ident")
+        make_identity(nc, ident[:])
+
+        window = psum.tile([P, S], F32, name="window")
+        nc.tensor.matmul(window[:], ident[:], base_sb[:], start=True, stop=False)
+
+        for e in range(E):
+            piece = offsets[:, e * QC : (e + 1) * QC]
+            for b in range(KB):
+                nc.tensor.matmul(
+                    window[:].indirect(piece),
+                    w_sb[:, e * KB + b, :],
+                    x_sb[:, b, e * Q : (e + 1) * Q],
+                    start=False,
+                    stop=(e == E - 1 and b == KB - 1),
+                )
+
+        z_sb = held.tile([P, S], F32, name="z_sb")
+        nc.vector.tensor_copy(z_sb[:], window[:])
+        nc.sync.dma_start(out, z_sb[:])

@@ -12,6 +12,8 @@ Q = 64
 N = E * Q
 QC = Q // 16
 
+CHUNKS = 2
+
 FLOPS = 2 * K * P * N
 
 
@@ -27,10 +29,10 @@ def tile_scatter_matmul_kernel(tc, base, x, w, offs, out):
         base_sb = held.tile([P, S], BF16, name="base_sb")
         nc.scalar.dma_start(base_sb[:], base)
 
-        w_sb = held.tile([P, E * KB, P], BF16, name="w_sb")
-        nc.sync.dma_start(w_sb[:], w.rearrange("e (b p) m -> p (e b) m", p=P))
+        w_sb = held.tile([P, E, KB, P], BF16, name="w_sb")
+        nc.sync.dma_start(w_sb[:], w.rearrange("e (p b) m -> p e b m", b=KB))
         x_sb = held.tile([P, KB, N], BF16, name="x_sb")
-        nc.scalar.dma_start(x_sb[:], x.rearrange("(b p) n -> p b n", p=P))
+        nc.scalar.dma_start(x_sb[:], x.rearrange("(p b) n -> p b n", b=KB))
 
         ident = held.tile([P, P], BF16, name="ident")
         make_identity(nc, ident[:])
@@ -43,12 +45,15 @@ def tile_scatter_matmul_kernel(tc, base, x, w, offs, out):
             for b in range(KB):
                 nc.tensor.matmul(
                     window[:].indirect(piece),
-                    w_sb[:, e * KB + b, :],
+                    w_sb[:, e, b, :],
                     x_sb[:, b, e * Q : (e + 1) * Q],
                     start=False,
                     stop=(e == E - 1 and b == KB - 1),
                 )
 
         z_sb = held.tile([P, S], F32, name="z_sb")
-        nc.vector.tensor_copy(z_sb[:], window[:])
-        nc.sync.dma_start(out, z_sb[:])
+        store_queues = (nc.sync, nc.scalar)
+        for c in range(CHUNKS):
+            cols = slice(c * (S // CHUNKS), (c + 1) * (S // CHUNKS))
+            nc.vector.tensor_copy(z_sb[:, cols], window[:, cols])
+            store_queues[c % 2].dma_start(out[:, cols], z_sb[:, cols])

@@ -12,7 +12,7 @@ Q = 64
 N = E * Q
 QC = Q // 16
 
-CHUNKS = 2
+WARM = 4
 
 FLOPS = 2 * K * P * N
 
@@ -29,10 +29,16 @@ def tile_scatter_matmul_kernel(tc, base, x, w, offs, out):
         base_sb = held.tile([P, S], BF16, name="base_sb")
         nc.scalar.dma_start(base_sb[:], base)
 
-        w_sb = held.tile([P, E, KB, P], BF16, name="w_sb")
-        nc.sync.dma_start(w_sb[:], w.rearrange("e (p b) m -> p e b m", b=KB))
+        w_sb = held.tile([P, E * KB, P], BF16, name="w_sb")
+        nc.sync.dma_start(w_sb[:], w.rearrange("e (b p) m -> p (e b) m", p=P))
         x_sb = held.tile([P, KB, N], BF16, name="x_sb")
-        nc.scalar.dma_start(x_sb[:], x.rearrange("(p b) n -> p b n", b=KB))
+        nc.scalar.dma_start(x_sb[:], x.rearrange("(b p) n -> p b n", p=P))
+
+        zeros = held.tile([P, S], BF16, name="zeros")
+        nc.vector.memset(zeros[:], 0.0)
+        unread = psum.tile([P, S], F32, name="unread")
+        for i in range(WARM):
+            nc.tensor.matmul(unread[:], zeros[:, 0:P], zeros[:], start=True, stop=True)
 
         ident = held.tile([P, P], BF16, name="ident")
         make_identity(nc, ident[:])
@@ -45,15 +51,12 @@ def tile_scatter_matmul_kernel(tc, base, x, w, offs, out):
             for b in range(KB):
                 nc.tensor.matmul(
                     window[:].indirect(piece),
-                    w_sb[:, e, b, :],
+                    w_sb[:, e * KB + b, :],
                     x_sb[:, b, e * Q : (e + 1) * Q],
                     start=False,
                     stop=(e == E - 1 and b == KB - 1),
                 )
 
         z_sb = held.tile([P, S], F32, name="z_sb")
-        store_queues = (nc.sync, nc.scalar)
-        for c in range(CHUNKS):
-            cols = slice(c * (S // CHUNKS), (c + 1) * (S // CHUNKS))
-            nc.vector.tensor_copy(z_sb[:, cols], window[:, cols])
-            store_queues[c % 2].dma_start(out[:, cols], z_sb[:, cols])
+        nc.vector.tensor_copy(z_sb[:], window[:])
+        nc.sync.dma_start(out, z_sb[:])

@@ -12,7 +12,7 @@ Q = 64
 N = E * Q
 QC = Q // 16
 
-WARM = 4
+WARM = 3
 
 FLOPS = 2 * K * P * N
 

@@ -13,6 +13,7 @@ N = E * Q
 QC = Q // 16
 
 WARM = 3
+CHUNKS = 2
 
 FLOPS = 2 * K * P * N
 
@@ -58,5 +59,7 @@ def tile_scatter_matmul_kernel(tc, base, x, w, offs, out):
                 )
 
         z_sb = held.tile([P, S], F32, name="z_sb")
-        nc.vector.tensor_copy(z_sb[:], window[:])
-        nc.sync.dma_start(out, z_sb[:])
+        for c in range(CHUNKS):
+            cols = slice(c * (S // CHUNKS), (c + 1) * (S // CHUNKS))
+            nc.vector.tensor_copy(z_sb[:, cols], window[:, cols])
+            nc.sync.dma_start(out[:, cols], z_sb[:, cols])

@@ -30,10 +30,10 @@ def tile_scatter_matmul_kernel(tc, base, x, w, offs, out):
         base_sb = held.tile([P, S], BF16, name="base_sb")
         nc.scalar.dma_start(base_sb[:], base)
 
-        w_sb = held.tile([P, E * KB, P], BF16, name="w_sb")
-        nc.sync.dma_start(w_sb[:], w.rearrange("e (b p) m -> p (e b) m", p=P))
+        w_sb = held.tile([P, E, KB, P], BF16, name="w_sb")
+        nc.sync.dma_start(w_sb[:], w.rearrange("e (p b) m -> p e b m", b=KB))
         x_sb = held.tile([P, KB, N], BF16, name="x_sb")
-        nc.scalar.dma_start(x_sb[:], x.rearrange("(b p) n -> p b n", p=P))
+        nc.scalar.dma_start(x_sb[:], x.rearrange("(p b) n -> p b n", b=KB))
 
         zeros = held.tile([P, S], BF16, name="zeros")
         nc.vector.memset(zeros[:], 0.0)
@@ -52,7 +52,7 @@ def tile_scatter_matmul_kernel(tc, base, x, w, offs, out):
             for b in range(KB):
                 nc.tensor.matmul(
                     window[:].indirect(piece),
-                    w_sb[:, e * KB + b, :],
+                    w_sb[:, e, b, :],
                     x_sb[:, b, e * Q : (e + 1) * Q],
                     start=False,
                     stop=(e == E - 1 and b == KB - 1),

@@ -24,16 +24,17 @@ def tile_scatter_matmul_kernel(tc, base, x, w, offs, out):
         tc.tile_pool(name="held", bufs=1) as held,
         tc.psum_pool(name="psum", bufs=1) as psum,
     ):
+        base_sb = held.tile([P, S], BF16, name="base_sb")
+        nc.sync.dma_start(base_sb[:], base)
+
+        x_sb = held.tile([P, KB, N], BF16, name="x_sb")
+        nc.sync.dma_start(x_sb[:], x.rearrange("(p b) n -> p b n", b=KB))
+
         offsets = held.tile([P, N // 16], U16, name="offsets")
         nc.sync.dma_start(offsets[:], offs)
 
-        base_sb = held.tile([P, S], BF16, name="base_sb")
-        nc.scalar.dma_start(base_sb[:], base)
-
         w_sb = held.tile([P, E, KB, P], BF16, name="w_sb")
         nc.sync.dma_start(w_sb[:], w.rearrange("e (p b) m -> p e b m", b=KB))
-        x_sb = held.tile([P, KB, N], BF16, name="x_sb")
-        nc.scalar.dma_start(x_sb[:], x.rearrange("(p b) n -> p b n", b=KB))
 
         zeros = held.tile([P, S], BF16, name="zeros")
         nc.vector.memset(zeros[:], 0.0)

@@ -13,7 +13,7 @@ N = E * Q
 QC = Q // 16
 
 WARM = 3
-CHUNKS = 2
+CHUNKS = 4
 
 FLOPS = 2 * K * P * N
 

@@ -13,7 +13,8 @@ N = E * Q
 QC = Q // 16
 
 WARM = 3
-CHUNKS = 4
+RUNS = (128, 192, 192)
+assert sum(RUNS) == S
 
 FLOPS = 2 * K * P * N
 
@@ -60,7 +61,9 @@ def tile_scatter_matmul_kernel(tc, base, x, w, offs, out):
                 )
 
         z_sb = held.tile([P, S], F32, name="z_sb")
-        for c in range(CHUNKS):
-            cols = slice(c * (S // CHUNKS), (c + 1) * (S // CHUNKS))
+        first = 0
+        for width in RUNS:
+            cols = slice(first, first + width)
             nc.vector.tensor_copy(z_sb[:, cols], window[:, cols])
             nc.sync.dma_start(out[:, cols], z_sb[:, cols])
+            first += width

@@ -35,7 +35,8 @@ def tile_scatter_matmul_kernel(tc, base, x, w, offs, out):
         nc.sync.dma_start(offsets[:], offs)
 
         w_sb = held.tile([P, E, KB, P], BF16, name="w_sb")
-        nc.sync.dma_start(w_sb[:], w.rearrange("e (p b) m -> p e b m", b=KB))
+        for e in range(E):
+            nc.sync.dma_start(w_sb[:, e], w[e].rearrange("(p b) m -> p b m", b=KB))
 
         zeros = held.tile([P, S], BF16, name="zeros")
         nc.vector.memset(zeros[:], 0.0)

@@ -12,7 +12,7 @@ Q = 64
 N = E * Q
 QC = Q // 16
 
-WARM = 3
+WARM = 16
 RUNS = (128, 192, 192)
 assert sum(RUNS) == S
 
@@ -38,11 +38,11 @@ def tile_scatter_matmul_kernel(tc, base, x, w, offs, out):
         for e in range(E):
             nc.sync.dma_start(w_sb[:, e], w[e].rearrange("(p b) m -> p b m", b=KB))
 
-        zeros = held.tile([P, S], BF16, name="zeros")
+        zeros = held.tile([P, P], BF16, name="zeros")
         nc.vector.memset(zeros[:], 0.0)
-        unread = psum.tile([P, S], F32, name="unread")
+        unread = psum.tile([P, P], F32, name="unread")
         for i in range(WARM):
-            nc.tensor.matmul(unread[:], zeros[:, 0:P], zeros[:], start=True, stop=True)
+            nc.tensor.matmul(unread[:], zeros[:], zeros[:], start=True, stop=True)
 
         ident = held.tile([P, P], BF16, name="ident")
         make_identity(nc, ident[:])

@@ -12,7 +12,7 @@ Q = 64
 N = E * Q
 QC = Q // 16
 
-WARM = 16
+WARM = 12
 RUNS = (128, 192, 192)
 assert sum(RUNS) == S
 

@@ -12,7 +12,7 @@ Q = 64
 N = E * Q
 QC = Q // 16
 
-WARM = 12
+WARM = 8
 RUNS = (128, 192, 192)
 assert sum(RUNS) == S
 

@@ -45,7 +45,8 @@ def tile_scatter_matmul_kernel(tc, base, x, w, offs, out):
             nc.tensor.matmul(unread[:], zeros[:], zeros[:], start=True, stop=True)
 
         ident = held.tile([P, P], BF16, name="ident")
-        make_identity(nc, ident[:])
+        nc.vector.memset(ident[:], 0.0)
+        make_identity(nc, ident[:], nomemset=True)
 
         window = psum.tile([P, S], F32, name="window")
         nc.tensor.matmul(window[:], ident[:], base_sb[:], start=True, stop=False)

@@ -12,7 +12,7 @@ Q = 64
 N = E * Q
 QC = Q // 16
 
-WARM = 8
+WARM = 10
 RUNS = (128, 192, 192)
 assert sum(RUNS) == S
 

@@ -13,7 +13,7 @@ N = E * Q
 QC = Q // 16
 
 WARM = 10
-RUNS = (128, 192, 192)
+RUNS = (128, 128, 256)
 assert sum(RUNS) == S
 
 FLOPS = 2 * K * P * N

import concourse.mybir as mybir
from concourse.masks import make_identity

BF16, F32, U16 = mybir.dt.bfloat16, mybir.dt.float32, mybir.dt.uint16

P = 128
S = 512
K = 256
KB = K // P
E = 2
Q = 64
N = E * Q
QC = Q // 16

WARM = 10
RUNS = (128, 128, 256)
assert sum(RUNS) == S

FLOPS = 2 * K * P * N


def tile_scatter_matmul_kernel(tc, base, x, w, offs, out):
    nc = tc.nc
    with (
        tc.tile_pool(name="held", bufs=1) as held,
        tc.psum_pool(name="psum", bufs=1) as psum,
    ):
        base_sb = held.tile([P, S], BF16, name="base_sb")
        nc.sync.dma_start(base_sb[:], base)

        x_sb = held.tile([P, KB, N], BF16, name="x_sb")
        nc.sync.dma_start(x_sb[:], x.rearrange("(p b) n -> p b n", b=KB))

        offsets = held.tile([P, N // 16], U16, name="offsets")
        nc.sync.dma_start(offsets[:], offs)

        w_sb = held.tile([P, E, KB, P], BF16, name="w_sb")
        for e in range(E):
            nc.sync.dma_start(w_sb[:, e], w[e].rearrange("(p b) m -> p b m", b=KB))

        zeros = held.tile([P, P], BF16, name="zeros")
        nc.vector.memset(zeros[:], 0.0)
        unread = psum.tile([P, P], F32, name="unread")
        for i in range(WARM):
            nc.tensor.matmul(unread[:], zeros[:], zeros[:], start=True, stop=True)

        ident = held.tile([P, P], BF16, name="ident")
        nc.vector.memset(ident[:], 0.0)
        make_identity(nc, ident[:], nomemset=True)

        window = psum.tile([P, S], F32, name="window")
        nc.tensor.matmul(window[:], ident[:], base_sb[:], start=True, stop=False)

        for e in range(E):
            piece = offsets[:, e * QC : (e + 1) * QC]
            for b in range(KB):
                nc.tensor.matmul(
                    window[:].indirect(piece),
                    w_sb[:, e, b, :],
                    x_sb[:, b, e * Q : (e + 1) * Q],
                    start=False,
                    stop=(e == E - 1 and b == KB - 1),
                )

        z_sb = held.tile([P, S], F32, name="z_sb")
        first = 0
        for width in RUNS:
            cols = slice(first, first + width)
            nc.vector.tensor_copy(z_sb[:, cols], window[:, cols])
            nc.sync.dma_start(out[:, cols], z_sb[:, cols])
            first += width
